import numpy as np
import ml_dtypes


def mxq(x, axis, fmt="e4m3"):
    dtype, down = {"e4m3": (ml_dtypes.float8_e4m3fn, 7), "e5m2": (ml_dtypes.float8_e5m2, 14)}[fmt]
    v = np.moveaxis(np.asarray(x, np.float32).astype(ml_dtypes.bfloat16).astype(np.float64), axis, -1)
    blocks = v.reshape(v.shape[:-1] + (-1, 32))
    amax = np.abs(blocks).max(-1, keepdims=True)
    byte = np.maximum(np.where(amax > 0, np.frexp(amax)[1] - 1 + 127, 0) - down, 1)
    scale = np.exp2(byte - 127.0)
    codes = (blocks / scale).astype(np.float32).astype(dtype).astype(np.float64)
    return np.moveaxis((codes * scale).reshape(v.shape), -1, axis)


WIDE = False


def mx_kscale(k):
    if not WIDE:
        return np.ones(k)
    levels = np.array([10, -10, 5, -5, 0])
    if k % 512:
        return np.exp2(np.random.permutation(np.resize(levels, k // 32))).repeat(32)
    a = np.empty((k // 512, 16))
    for p in range(k // 512):
        a[p, :8] = np.random.permutation(np.resize(levels, 8))
        for g in range(8):
            far = levels[np.abs(levels - a[p, g]) >= 10]
            a[p, g + 8] = far[np.random.randint(len(far))]
    return np.exp2(a.ravel()).repeat(32)


def f64(x):
    return np.asarray(x).astype(np.float64)


def striped(idx):
    return np.tile(np.asarray(idx).reshape(-1, 16).T, (8, 1)).astype(np.uint16)


def unstriped(offs):
    return offs[:16].T.reshape(-1).astype(np.int64)


E2M1 = np.array([0.0, 0.5, 1.0, 1.5, 2.0, 3.0, 4.0, 6.0, -0.0, -0.5, -1.0, -1.5, -2.0, -3.0, -4.0, -6.0])


def pack_weight(w, fmt):
    k, n = w.shape
    w = f64(np.asarray(w, np.float32).astype(ml_dtypes.bfloat16)).reshape(k // 32, 32, n)
    amax = np.abs(w).max(1)
    if fmt == "e4m3":
        byte = np.frexp(amax)[1] - 1 + 127 - 7
    else:
        mant, ex = np.frexp(amax / 6.0)
        byte = np.where(mant > 0.5, ex, ex - 1) + 127
    byte = np.clip(np.where(amax > 0, byte, 1), 1, 254)
    scaled = (w * np.exp2(127.0 - byte)[:, None, :]).reshape(k, n).astype(np.float32)
    by_word = np.ascontiguousarray(scaled.reshape(k // 512, 128, 4, n).transpose(0, 1, 3, 2))
    if fmt == "e4m3":
        words = by_word.astype(ml_dtypes.float8_e4m3fn).view(np.uint8)
    else:
        c = by_word.astype(ml_dtypes.float4_e2m1fn).view(np.uint8) & 0xF
        words = (c[..., 0::2] | (c[..., 1::2] << 4)).reshape(k // 512, 128, 2 * n)
    return np.ascontiguousarray(words), np.ascontiguousarray(byte.astype(np.uint8).reshape(k // 512, 16, n))


def unpack_weight(words, scales, fmt):
    g, _, n = scales.shape
    words = np.ascontiguousarray(words).reshape(g, 128, n, -1)
    if fmt == "e4m3":
        vals = words.view(ml_dtypes.float8_e4m3fn).astype(np.float64)
    else:
        nib = np.empty((g, 128, n, 4), np.uint8)
        nib[..., 0::2] = words & 0xF
        nib[..., 1::2] = words >> 4
        vals = E2M1[nib]
    vals = vals * np.repeat(np.exp2(scales.astype(np.float64) - 127.0), 8, axis=1)[..., None]
    return vals.transpose(0, 1, 3, 2).reshape(g * 512, n)


def sigmoid(v):
    return 1.0 / (1.0 + np.exp(-v))


D, E, T, I, Q = 512, 512, 2048, 512, 128


def setup_inputs():
    n = np.random.standard_normal
    idx = np.random.permutation(T)[:I]
    fd = mx_kscale(D)
    fe = mx_kscale(E)
    keysp = pack_weight(n((D, T)) / fd[:, None], "e4m3")
    valsp = pack_weight(n((E, T)) / fe[:, None], "e4m3")
    return {
        "query": (n((D, Q)) * 0.8 / np.sqrt(D) * fd[:, None]).astype(np.float32),
        "keys_words": keysp[0],
        "keys_scales": keysp[1],
        "th": (np.random.uniform(5.8, 6.1, (Q, 1))).astype(np.float32),
        "steep": (np.random.uniform(1.0, 4.0, (Q, 1))).astype(np.float32),
        "sdot": (np.random.uniform(-0.3, 0.3, (Q, 1))).astype(np.float32),
        "gout": (n((E, Q)) * 1 / np.sqrt(E) * fe[:, None]).astype(np.float32),
        "vals_words": valsp[0],
        "vals_scales": valsp[1],
        "old": (0.5 * n((Q, T))).astype(np.float32),
        "offs": striped(idx),
    }


def reference(query, keys_words, keys_scales, th, steep, sdot, gout, vals_words, vals_scales, old, offs):
    idx = unstriped(offs)
    keysu = unpack_weight(keys_words, keys_scales, "e4m3")
    valsu = unpack_weight(vals_words, vals_scales, "e4m3")
    queryq = mxq(f64(query), 0, "e4m3")
    keysidxg = keysu[:, idx]
    a = queryq.T @ keysidxg
    b = a - np.max(a, axis=1, keepdims=True)
    p = np.exp(b)
    z = np.sum(p, axis=1, keepdims=True)
    en = np.log(z) - np.sum(p * b, axis=1, keepdims=True) / z
    gt = sigmoid((f64(th) - en) * f64(steep))
    goutq = mxq(f64(gout), 0, "e4m3")
    valsidxg = valsu[:, idx]
    c0 = goutq.T @ valsidxg
    dgt = np.sum(p * c0, axis=1, keepdims=True) / z - f64(sdot)
    den = dgt * gt * (1.0 - gt) * f64(steep) * (-1.0)
    dz = den / z - gt * np.sum(p * c0, axis=1, keepdims=True) / np.square(z) - den * (-1.0) * np.sum(p * b, axis=1, keepdims=True) / np.square(z)
    dp = gt / z * c0 + den * (-1.0) / z * b + dz
    db = den * (-1.0) / z * p + dp * p
    gs = db * 1024.0
    gf = np.zeros((Q, T))
    gf[:, idx] = gs
    y = f64(old) + gf
    return y

@@ -1,0 +1,188 @@
+import math
+from contextlib import ExitStack
+
+import concourse.mybir as mybir
+
+F32 = mybir.dt.float32
+BF16 = mybir.dt.bfloat16
+I32 = mybir.dt.int32
+U32 = mybir.dt.uint32
+U16 = mybir.dt.uint16
+U8 = mybir.dt.uint8
+FP8X4 = mybir.dt.float8_e4m3fn_x4
+ALU = mybir.AluOpType
+ACT = mybir.ActivationFunctionType
+
+P = 128
+PACK = 4
+TOKENS = 2048
+SLOTS = 512
+ROWS = 128
+FLOPS = 2 * 2 * 512 * ROWS * SLOTS
+
+GRAD_SCALE = 1024.0
+LN2 = math.log(2.0)
+GUESS_SLOPE = LN2 / 2.0**23
+GUESS_SHIFT = 127.0 * LN2 - 0.03
+STORE_WIDTHS = (256, 512, 512, 512, 256)
+
+
+def tile_attend_bcertainty_s_kernel(tc, query, keys_words, keys_scales, th, steep, sdot, gout,
+                                     vals_words, vals_scales, old, offs, out):
+    nc = tc.nc
+    with ExitStack() as ctx:
+        keep = ctx.enter_context(tc.tile_pool(name="keep", bufs=1))
+        psum = ctx.enter_context(tc.psum_pool(name="psum", bufs=1))
+
+        def column(name):
+            return keep.tile([P, 1], F32, name=name)
+
+        def affine(name, x, scale, bias, func=ACT.Identity):
+            y = column(name)
+            nc.scalar.activation(out=y[:], in_=x, func=func, scale=scale, bias=bias)
+            return y
+
+        def times(name, x, scale):
+            y = column(name)
+            nc.scalar.activation(out=y[:], in_=x, func=ACT.Copy, scale=scale)
+            return y
+
+        offsets = keep.tile([P, SLOTS // 16], U16, name="offsets")
+        nc.sync.dma_start(offsets[:], offs)
+
+        def load_operand(src):
+            raw = keep.tile([P, PACK, ROWS], F32, name="raw", tag="raw")
+            nc.sync.dma_start(out=raw[:], in_=src.rearrange("(p j) w -> p j w", j=PACK))
+            return raw
+
+        def quantize(name, tag, raw):
+            grouped = keep.tile([P, ROWS, PACK], BF16, name=name + "_grouped", tag=tag, align_bytes=64)
+            nc.scalar.copy(out=grouped[:], in_=raw[:].rearrange("p j w -> p w j"))
+            codes = keep.tile([P, ROWS], U32, name=name + "_codes", align_bytes=64)
+            scales = keep.tile([P, ROWS], U8, name=name + "_scales", align_bytes=64)
+            nc.vector.quantize_mx(out=codes[:].bitcast(FP8X4), scales=scales[:],
+                                  in_=grouped[:].rearrange("p w j -> p (w j)"))
+            return codes, scales
+
+        def load_words(name, tag, src):
+            words = keep.tile([P, TOKENS], I32, name=name, tag=tag, align_bytes=64)
+            nc.sync.dma_start(out=words[:], in_=src[0].rearrange("p n t -> p (n t)").bitcast(I32))
+            return words
+
+        def load_plane(name, tag, src):
+            plane = keep.tile([P, TOKENS], U8, name=name, tag=tag)
+            nc.vector.memset(plane[:].bitcast(I32), 0)
+            for quad in range(4):
+                nc.sync.dma_start(out=plane[32 * quad : 32 * quad + 4, :].bitcast(I32),
+                                  in_=src[0, 4 * quad : 4 * quad + 4, :].bitcast(I32))
+            return plane
+
+        def gather(name, window, dtype):
+            picked = keep.tile([P, SLOTS], dtype, name=name, align_bytes=64)
+            nc.vector.tensor_copy(picked[:], window.indirect(offsets[:]))
+            return picked
+
+        def product(name, stationary, words, plane):
+            acc = psum.tile([ROWS, SLOTS], F32, name=name)
+            nc.tensor.matmul_mx(out=acc[:], lhsT=stationary[0][:].bitcast(FP8X4), lhsT_scale=stationary[1][:],
+                                rhs=words[:].bitcast(FP8X4), rhs_scale=plane[:], start=True, stop=True)
+            return acc
+
+        q_raw = load_operand(query)
+        one = keep.tile([P, 1], F32, name="one", tag="k_pool", align_bytes=64)
+        nc.vector.memset(one[:], 1.0)
+        k_plane = load_plane("k_plane", "k_plane", keys_scales)
+
+        consts = keep.tile([P, 3], F32, name="consts")
+        for j, c in enumerate((2.0, GUESS_SHIFT, GUESS_SHIFT - 0.5)):
+            nc.vector.tensor_scalar(out=consts[:, j : j + 1], in0=one[:], scalar1=c, scalar2=None, op0=ALU.mult)
+        two, guess_e, guess_s = [consts[:, j : j + 1] for j in range(3)]
+        k_pool = load_words("k_pool", "k_pool", keys_words)
+        v_plane = load_plane("v_plane", "v_plane", vals_scales)
+
+        window = keep.tile([ROWS, TOKENS], F32, name="window")
+        nc.vector.memset(window[:].bitcast(I32), 0)
+
+        row_in = {}
+        for name, src in (("steep", steep), ("th", th), ("sdot", sdot)):
+            row_in[name] = column(name)
+            nc.gpsimd.dma_start(out=row_in[name][:], in_=src)
+
+
+        k_bytes = gather("k_bytes", k_plane[:], U8)
+        q_mx = quantize("q", "shared", q_raw)
+        g_raw = load_operand(gout)
+        v_pool = load_words("v_pool", "shared", vals_words)
+        k_words = gather("k_words", k_pool[:].bitcast(U32), U32)
+        a = product("a", q_mx, k_words, k_bytes)
+        v_bytes = gather("v_bytes", v_plane[:], U8)
+        g_mx = quantize("g", "g_grouped", g_raw)
+
+        steeps = keep.tile([P, 4], F32, name="steeps")
+        for j, c in enumerate((0.5, -0.5, 0.25, -0.25)):
+            nc.gpsimd.tensor_scalar(out=steeps[:, j : j + 1], in0=row_in["steep"][:], scalar1=c, scalar2=0.0,
+                                    op0=ALU.mult, op1=ALU.add)
+        neg_half, quarter, neg_quarter = [steeps[:, j : j + 1] for j in (1, 2, 3)]
+
+        neg_max = column("neg_max")
+        nc.vector.tensor_reduce(out=neg_max[:], in_=a[:], axis=mybir.AxisListType.X, op=ALU.max, negate=True)
+        p = keep.tile([ROWS, SLOTS], F32, name="p", tag="raw")
+        z = column("z")
+        nc.scalar.activation(out=p[:], in_=a[:], func=ACT.Exp, bias=neg_max[:], scale=1.0, accum_out=z[:])
+
+        v_words = gather("v_words", v_pool[:].bitcast(U32), U32)
+        c0 = product("c0", g_mx, v_words, v_bytes)
+        old_sb = keep.tile([ROWS, TOKENS], F32, name="old_sb", tag="shared", align_bytes=64)
+        nc.sync.dma_start(out=old_sb[:], in_=old)
+
+        r = column("r")
+        nc.vector.reciprocal(out=r[:], in_=z[:])
+        pb = keep.tile([ROWS, SLOTS], F32, name="pb")
+        sum_pb = column("sum_pb")
+        nc.vector.scalar_tensor_tensor(out=pb[:], in0=a[:], scalar=neg_max[:], in1=p[:], op0=ALU.add,
+                                       op1=ALU.mult, accum_out=sum_pb[:])
+        pc = keep.tile([ROWS, SLOTS], F32, name="pc")
+        sum_pc = column("sum_pc")
+        nc.vector.scalar_tensor_tensor(out=pc[:], in0=c0[:], scalar=row_in["sdot"][:], in1=p[:],
+                                       op0=ALU.subtract, op1=ALU.mult, accum_out=sum_pc[:])
+
+        z_bits = z[:].bitcast(U32)
+        e0 = affine("e0", z_bits, -GUESS_SLOPE, guess_e, ACT.Exp)
+        neg_z = times("neg_z", z[:], -1.0)
+        shift = affine("shift", z_bits, -GUESS_SLOPE, guess_s)
+        sq0 = affine("sq0", e0[:], neg_z[:], two, ACT.Square)
+        shift_th = affine("shift_th", shift[:], 1.0, row_in["th"][:])
+        e1 = affine("e1", sq0[:], 0.5, shift[:], ACT.Exp)
+        shift_term = affine("shift_term", shift_th[:], neg_half, quarter)
+        by_z = keep.tile([P, 2], F32, name="by_z")
+        nc.scalar.activation(out=by_z[:], in_=steeps[:, 0:2], func=ACT.Copy, scale=r[:])
+        half_r, neg_half_r = by_z[:, 0:1], by_z[:, 1:2]
+        sq1 = affine("sq1", e1[:], neg_z[:], two, ACT.Square)
+        sq0_term = affine("sq0_term", sq0[:], neg_quarter, shift_term[:])
+        neg_r = times("neg_r", r[:], -1.0)
+        gate_bias = affine("gate_bias", sum_pb[:], neg_half_r, sq0_term[:])
+        mean_b = times("mean_b", sum_pb[:], r[:])
+        t = affine("t", sq1[:], neg_quarter, gate_bias[:], ACT.Tanh)
+        n1 = times("n1", mean_b[:], neg_half_r)
+        n2 = affine("n2", mean_b[:], neg_half_r, neg_r[:])
+        d0 = affine("d0", t[:], half_r, half_r)
+        d1 = affine("d1", t[:], n1[:], n2[:])
+        neg_beta = times("neg_beta", d1[:], sum_pc[:])
+        gate_r = affine("gate_r", t[:], neg_r[:], r[:])
+        row_scale = times("row_scale", gate_r[:], GRAD_SCALE / 2)
+
+        b_term = keep.tile([ROWS, SLOTS], F32, name="b_term")
+        nc.vector.tensor_scalar(out=b_term[:], in0=pb[:], scalar1=d0[:], scalar2=sum_pc[:], op0=ALU.mult, op1=ALU.mult)
+        c_term = keep.tile([ROWS, SLOTS], F32, name="c_term")
+        nc.vector.scalar_tensor_tensor(out=c_term[:], in0=p[:], scalar=neg_beta[:], in1=pc[:], op0=ALU.mult, op1=ALU.add)
+        nc.vector.tensor_tensor(window[:].indirect(offsets[:]), b_term[:], c_term[:], ALU.add)
+
+        start = 0
+        for i, width in enumerate(STORE_WIDTHS):
+            cols = slice(start, start + width)
+            start = start + width
+            result = keep.tile([ROWS, width], F32, name="result%d" % i)
+            nc.vector.scalar_tensor_tensor(out=result[:], in0=window[:, cols], scalar=row_scale[:],
+                                           in1=old_sb[:, cols], op0=ALU.mult, op1=ALU.add)
+            queue = nc.sync if i % 2 == 0 else nc.scalar
+            queue.dma_start(out=out[:, cols], in_=result[:])

@@ -24,7 +24,7 @@ GRAD_SCALE = 1024.0
 LN2 = math.log(2.0)
 GUESS_SLOPE = LN2 / 2.0**23
 GUESS_SHIFT = 127.0 * LN2 - 0.03
-STORE_WIDTHS = (256, 512, 512, 512, 256)
+STORE_WIDTHS = (256, 384, 384, 384, 384, 256)
 
 
 def tile_attend_bcertainty_s_kernel(tc, query, keys_words, keys_scales, th, steep, sdot, gout,
@@ -50,8 +50,8 @@ def tile_attend_bcertainty_s_kernel(tc, query, keys_words, keys_scales, th, stee
         offsets = keep.tile([P, SLOTS // 16], U16, name="offsets")
         nc.sync.dma_start(offsets[:], offs)
 
-        def load_operand(src):
-            raw = keep.tile([P, PACK, ROWS], F32, name="raw", tag="raw")
+        def load_operand(name, src):
+            raw = keep.tile([P, PACK, ROWS], F32, name=name, tag=name, align_bytes=64)
             nc.sync.dma_start(out=raw[:], in_=src.rearrange("(p j) w -> p j w", j=PACK))
             return raw
 
@@ -88,7 +88,8 @@ def tile_attend_bcertainty_s_kernel(tc, query, keys_words, keys_scales, th, stee
                                 rhs=words[:].bitcast(FP8X4), rhs_scale=plane[:], start=True, stop=True)
             return acc
 
-        q_raw = load_operand(query)
+        q_raw = load_operand("q_raw", query)
+        g_raw = load_operand("g_raw", gout)
         one = keep.tile([P, 1], F32, name="one", tag="k_pool", align_bytes=64)
         nc.vector.memset(one[:], 1.0)
         k_plane = load_plane("k_plane", "k_plane", keys_scales)
@@ -110,13 +111,12 @@ def tile_attend_bcertainty_s_kernel(tc, query, keys_words, keys_scales, th, stee
 
 
         k_bytes = gather("k_bytes", k_plane[:], U8)
-        q_mx = quantize("q", "shared", q_raw)
-        g_raw = load_operand(gout)
-        v_pool = load_words("v_pool", "shared", vals_words)
+        q_mx = quantize("q", "q_grouped", q_raw)
+        g_mx = quantize("g", "g_grouped", g_raw)
+        v_pool = load_words("v_pool", "q_raw", vals_words)
         k_words = gather("k_words", k_pool[:].bitcast(U32), U32)
         a = product("a", q_mx, k_words, k_bytes)
         v_bytes = gather("v_bytes", v_plane[:], U8)
-        g_mx = quantize("g", "g_grouped", g_raw)
 
         steeps = keep.tile([P, 4], F32, name="steeps")
         for j, c in enumerate((0.5, -0.5, 0.25, -0.25)):
@@ -124,22 +124,22 @@ def tile_attend_bcertainty_s_kernel(tc, query, keys_words, keys_scales, th, stee
                                     op0=ALU.mult, op1=ALU.add)
         neg_half, quarter, neg_quarter = [steeps[:, j : j + 1] for j in (1, 2, 3)]
 
-        neg_max = column("neg_max")
+        neg_max = keep.tile([P, 1], F32, name="neg_max", tag="v_plane")
         nc.vector.tensor_reduce(out=neg_max[:], in_=a[:], axis=mybir.AxisListType.X, op=ALU.max, negate=True)
-        p = keep.tile([ROWS, SLOTS], F32, name="p", tag="raw")
+        p = keep.tile([ROWS, SLOTS], F32, name="p")
         z = column("z")
         nc.scalar.activation(out=p[:], in_=a[:], func=ACT.Exp, bias=neg_max[:], scale=1.0, accum_out=z[:])
 
         v_words = gather("v_words", v_pool[:].bitcast(U32), U32)
         c0 = product("c0", g_mx, v_words, v_bytes)
-        old_sb = keep.tile([ROWS, TOKENS], F32, name="old_sb", tag="shared", align_bytes=64)
+        old_sb = keep.tile([ROWS, TOKENS], F32, name="old_sb", tag="k_pool", align_bytes=64)
         nc.sync.dma_start(out=old_sb[:], in_=old)
 
-        r = column("r")
-        nc.vector.reciprocal(out=r[:], in_=z[:])
-        pb = keep.tile([ROWS, SLOTS], F32, name="pb")
+        pb_r = keep.tile([ROWS, SLOTS + 1], F32, name="pb_r", tag="q_raw", align_bytes=64)
+        pb, r = pb_r[:, :SLOTS], pb_r[:, SLOTS:]
+        nc.vector.reciprocal(out=r, in_=z[:])
         sum_pb = column("sum_pb")
-        nc.vector.scalar_tensor_tensor(out=pb[:], in0=a[:], scalar=neg_max[:], in1=p[:], op0=ALU.add,
+        nc.vector.scalar_tensor_tensor(out=pb, in0=a[:], scalar=neg_max[:], in1=p[:], op0=ALU.add,
                                        op1=ALU.mult, accum_out=sum_pb[:])
         pc = keep.tile([ROWS, SLOTS], F32, name="pc")
         sum_pc = column("sum_pc")
@@ -155,24 +155,24 @@ def tile_attend_bcertainty_s_kernel(tc, query, keys_words, keys_scales, th, stee
         e1 = affine("e1", sq0[:], 0.5, shift[:], ACT.Exp)
         shift_term = affine("shift_term", shift_th[:], neg_half, quarter)
         by_z = keep.tile([P, 2], F32, name="by_z")
-        nc.scalar.activation(out=by_z[:], in_=steeps[:, 0:2], func=ACT.Copy, scale=r[:])
+        nc.scalar.activation(out=by_z[:], in_=steeps[:, 0:2], func=ACT.Copy, scale=r)
         half_r, neg_half_r = by_z[:, 0:1], by_z[:, 1:2]
         sq1 = affine("sq1", e1[:], neg_z[:], two, ACT.Square)
         sq0_term = affine("sq0_term", sq0[:], neg_quarter, shift_term[:])
-        neg_r = times("neg_r", r[:], -1.0)
+        neg_r = times("neg_r", r, -1.0)
         gate_bias = affine("gate_bias", sum_pb[:], neg_half_r, sq0_term[:])
-        mean_b = times("mean_b", sum_pb[:], r[:])
+        mean_b = times("mean_b", sum_pb[:], r)
         t = affine("t", sq1[:], neg_quarter, gate_bias[:], ACT.Tanh)
         n1 = times("n1", mean_b[:], neg_half_r)
         n2 = affine("n2", mean_b[:], neg_half_r, neg_r[:])
         d0 = affine("d0", t[:], half_r, half_r)
         d1 = affine("d1", t[:], n1[:], n2[:])
         neg_beta = times("neg_beta", d1[:], sum_pc[:])
-        gate_r = affine("gate_r", t[:], neg_r[:], r[:])
+        gate_r = affine("gate_r", t[:], neg_r[:], r)
         row_scale = times("row_scale", gate_r[:], GRAD_SCALE / 2)
 
         b_term = keep.tile([ROWS, SLOTS], F32, name="b_term")
-        nc.vector.tensor_scalar(out=b_term[:], in0=pb[:], scalar1=d0[:], scalar2=sum_pc[:], op0=ALU.mult, op1=ALU.mult)
+        nc.vector.tensor_scalar(out=b_term[:], in0=pb, scalar1=d0[:], scalar2=sum_pc[:], op0=ALU.mult, op1=ALU.mult)
         c_term = keep.tile([ROWS, SLOTS], F32, name="c_term")
         nc.vector.scalar_tensor_tensor(out=c_term[:], in0=p[:], scalar=neg_beta[:], in1=pc[:], op0=ALU.mult, op1=ALU.add)
         nc.vector.tensor_tensor(window[:].indirect(offsets[:]), b_term[:], c_term[:], ALU.add)

@@ -69,12 +69,11 @@ def tile_attend_bcertainty_s_kernel(tc, query, keys_words, keys_scales, th, stee
             nc.sync.dma_start(out=words[:], in_=src[0].rearrange("p n t -> p (n t)").bitcast(I32))
             return words
 
-        def load_plane(name, tag, src):
+        def load_plane(name, tag, src, first):
             plane = keep.tile([P, TOKENS], U8, name=name, tag=tag)
             nc.vector.memset(plane[:].bitcast(I32), 0)
-            for quad in range(4):
-                nc.sync.dma_start(out=plane[32 * quad : 32 * quad + 4, :].bitcast(I32),
-                                  in_=src[0, 4 * quad : 4 * quad + 4, :].bitcast(I32))
+            for j in range(4):
+                nc.sync.dma_start(out=plane[first + j : P : 32, :].bitcast(I32), in_=src[0, j:16:4, :].bitcast(I32))
             return plane
 
         def gather(name, window, dtype):
@@ -85,21 +84,21 @@ def tile_attend_bcertainty_s_kernel(tc, query, keys_words, keys_scales, th, stee
         def product(name, stationary, words, plane):
             acc = psum.tile([ROWS, SLOTS], F32, name=name)
             nc.tensor.matmul_mx(out=acc[:], lhsT=stationary[0][:].bitcast(FP8X4), lhsT_scale=stationary[1][:],
-                                rhs=words[:].bitcast(FP8X4), rhs_scale=plane[:], start=True, stop=True)
+                                rhs=words[:].bitcast(FP8X4), rhs_scale=plane, start=True, stop=True)
             return acc
 
         q_raw = load_operand("q_raw", query)
         g_raw = load_operand("g_raw", gout)
         one = keep.tile([P, 1], F32, name="one", tag="k_pool", align_bytes=64)
         nc.vector.memset(one[:], 1.0)
-        k_plane = load_plane("k_plane", "k_plane", keys_scales)
+        k_plane = load_plane("k_plane", "k_plane", keys_scales, 0)
 
         consts = keep.tile([P, 3], F32, name="consts")
         for j, c in enumerate((2.0, GUESS_SHIFT, GUESS_SHIFT - 0.5)):
             nc.vector.tensor_scalar(out=consts[:, j : j + 1], in0=one[:], scalar1=c, scalar2=None, op0=ALU.mult)
         two, guess_e, guess_s = [consts[:, j : j + 1] for j in range(3)]
         k_pool = load_words("k_pool", "k_pool", keys_words)
-        v_plane = load_plane("v_plane", "v_plane", vals_scales)
+        v_plane = load_plane("v_plane", "v_plane", vals_scales, 4)
 
         window = keep.tile([ROWS, TOKENS], F32, name="window")
         nc.vector.memset(window[:].bitcast(I32), 0)
@@ -115,7 +114,7 @@ def tile_attend_bcertainty_s_kernel(tc, query, keys_words, keys_scales, th, stee
         g_mx = quantize("g", "g_grouped", g_raw)
         v_pool = load_words("v_pool", "q_raw", vals_words)
         k_words = gather("k_words", k_pool[:].bitcast(U32), U32)
-        a = product("a", q_mx, k_words, k_bytes)
+        a = product("a", q_mx, k_words, k_bytes[:])
         v_bytes = gather("v_bytes", v_plane[:], U8)
 
         steeps = keep.tile([P, 4], F32, name="steeps")
@@ -131,7 +130,7 @@ def tile_attend_bcertainty_s_kernel(tc, query, keys_words, keys_scales, th, stee
         nc.scalar.activation(out=p[:], in_=a[:], func=ACT.Exp, bias=neg_max[:], scale=1.0, accum_out=z[:])
 
         v_words = gather("v_words", v_pool[:].bitcast(U32), U32)
-        c0 = product("c0", g_mx, v_words, v_bytes)
+        c0 = product("c0", g_mx, v_words, v_bytes[4:P, :])
         old_sb = keep.tile([ROWS, TOKENS], F32, name="old_sb", tag="k_pool", align_bytes=64)
         nc.sync.dma_start(out=old_sb[:], in_=old)
 

@@ -69,6 +69,11 @@ def tile_attend_bcertainty_s_kernel(tc, query, keys_words, keys_scales, th, stee
             nc.sync.dma_start(out=words[:], in_=src[0].rearrange("p n t -> p (n t)").bitcast(I32))
             return words
 
+        def load_column(name, tag, src):
+            col = keep.tile([P, 1], F32, name=name, tag=tag, align_bytes=64)
+            nc.sync.dma_start(out=col[:], in_=src)
+            return col
+
         def load_plane(name, tag, src, first):
             plane = keep.tile([P, TOKENS], U8, name=name, tag=tag)
             nc.vector.memset(plane[:].bitcast(I32), 0)
@@ -94,38 +99,37 @@ def tile_attend_bcertainty_s_kernel(tc, query, keys_words, keys_scales, th, stee
         k_plane = load_plane("k_plane", "k_plane", keys_scales, 0)
 
         consts = keep.tile([P, 3], F32, name="consts")
-        for j, c in enumerate((2.0, GUESS_SHIFT, GUESS_SHIFT - 0.5)):
+        for j, c in enumerate((-2.0, GUESS_SHIFT, GUESS_SHIFT - 0.5)):
             nc.vector.tensor_scalar(out=consts[:, j : j + 1], in0=one[:], scalar1=c, scalar2=None, op0=ALU.mult)
-        two, guess_e, guess_s = [consts[:, j : j + 1] for j in range(3)]
+        neg_two, guess_e, guess_s = [consts[:, j : j + 1] for j in range(3)]
         k_pool = load_words("k_pool", "k_pool", keys_words)
         v_plane = load_plane("v_plane", "v_plane", vals_scales, 4)
 
         window = keep.tile([ROWS, TOKENS], F32, name="window")
         nc.vector.memset(window[:].bitcast(I32), 0)
 
-        row_in = {}
-        for name, src in (("steep", steep), ("th", th), ("sdot", sdot)):
-            row_in[name] = column(name)
-            nc.gpsimd.dma_start(out=row_in[name][:], in_=src)
-
 
         k_bytes = gather("k_bytes", k_plane[:], U8)
         q_mx = quantize("q", "q_grouped", q_raw)
         g_mx = quantize("g", "g_grouped", g_raw)
-        v_pool = load_words("v_pool", "q_raw", vals_words)
+        steep_sb = load_column("steep_sb", "q_raw", steep)
+        v_pool = load_words("v_pool", "g_raw", vals_words)
+        th_sb = load_column("th_sb", "q_grouped", th)
+        sdot_sb = load_column("sdot_sb", "g_grouped", sdot)
         k_words = gather("k_words", k_pool[:].bitcast(U32), U32)
         a = product("a", q_mx, k_words, k_bytes[:])
         v_bytes = gather("v_bytes", v_plane[:], U8)
 
-        steeps = keep.tile([P, 4], F32, name="steeps")
-        for j, c in enumerate((0.5, -0.5, 0.25, -0.25)):
-            nc.gpsimd.tensor_scalar(out=steeps[:, j : j + 1], in0=row_in["steep"][:], scalar1=c, scalar2=0.0,
-                                    op0=ALU.mult, op1=ALU.add)
-        neg_half, quarter, neg_quarter = [steeps[:, j : j + 1] for j in (1, 2, 3)]
+        steeps = keep.tile([P, 5], F32, name="steeps")
+        for j, c in enumerate((0.25, -0.25, 0.5, -0.5)):
+            nc.scalar.activation(out=steeps[:, j : j + 1], in_=steep_sb[:], func=ACT.Copy, scale=c)
+        nc.scalar.activation(out=steeps[:, 4:5], in_=neg_two, func=ACT.Copy, scale=0.5)
+        quarter, neg_quarter, neg_half = [steeps[:, j : j + 1] for j in (0, 1, 3)]
+        th_term = affine("th_term", th_sb[:], neg_half, quarter)
 
         neg_max = keep.tile([P, 1], F32, name="neg_max", tag="v_plane")
         nc.vector.tensor_reduce(out=neg_max[:], in_=a[:], axis=mybir.AxisListType.X, op=ALU.max, negate=True)
-        p = keep.tile([ROWS, SLOTS], F32, name="p")
+        p = keep.tile([ROWS, SLOTS], F32, name="p", tag="q_raw", align_bytes=64)
         z = column("z")
         nc.scalar.activation(out=p[:], in_=a[:], func=ACT.Exp, bias=neg_max[:], scale=1.0, accum_out=z[:])
 
@@ -134,7 +138,7 @@ def tile_attend_bcertainty_s_kernel(tc, query, keys_words, keys_scales, th, stee
         old_sb = keep.tile([ROWS, TOKENS], F32, name="old_sb", tag="k_pool", align_bytes=64)
         nc.sync.dma_start(out=old_sb[:], in_=old)
 
-        pb_r = keep.tile([ROWS, SLOTS + 1], F32, name="pb_r", tag="q_raw", align_bytes=64)
+        pb_r = keep.tile([ROWS, SLOTS + 1], F32, name="pb_r", tag="g_raw", align_bytes=64)
         pb, r = pb_r[:, :SLOTS], pb_r[:, SLOTS:]
         nc.vector.reciprocal(out=r, in_=z[:])
         sum_pb = column("sum_pb")
@@ -142,32 +146,29 @@ def tile_attend_bcertainty_s_kernel(tc, query, keys_words, keys_scales, th, stee
                                        op1=ALU.mult, accum_out=sum_pb[:])
         pc = keep.tile([ROWS, SLOTS], F32, name="pc")
         sum_pc = column("sum_pc")
-        nc.vector.scalar_tensor_tensor(out=pc[:], in0=c0[:], scalar=row_in["sdot"][:], in1=p[:],
+        nc.vector.scalar_tensor_tensor(out=pc[:], in0=c0[:], scalar=sdot_sb[:], in1=p[:],
                                        op0=ALU.subtract, op1=ALU.mult, accum_out=sum_pc[:])
 
         z_bits = z[:].bitcast(U32)
         e0 = affine("e0", z_bits, -GUESS_SLOPE, guess_e, ACT.Exp)
-        neg_z = times("neg_z", z[:], -1.0)
         shift = affine("shift", z_bits, -GUESS_SLOPE, guess_s)
-        sq0 = affine("sq0", e0[:], neg_z[:], two, ACT.Square)
-        shift_th = affine("shift_th", shift[:], 1.0, row_in["th"][:])
+        sq0 = affine("sq0", e0[:], z[:], neg_two, ACT.Square)
+        shift_term = affine("shift_term", shift[:], neg_half, th_term[:])
         e1 = affine("e1", sq0[:], 0.5, shift[:], ACT.Exp)
-        shift_term = affine("shift_term", shift_th[:], neg_half, quarter)
-        by_z = keep.tile([P, 2], F32, name="by_z")
-        nc.scalar.activation(out=by_z[:], in_=steeps[:, 0:2], func=ACT.Copy, scale=r)
-        half_r, neg_half_r = by_z[:, 0:1], by_z[:, 1:2]
-        sq1 = affine("sq1", e1[:], neg_z[:], two, ACT.Square)
         sq0_term = affine("sq0_term", sq0[:], neg_quarter, shift_term[:])
-        neg_r = times("neg_r", r, -1.0)
+        by_z = keep.tile([P, 3], F32, name="by_z")
+        nc.scalar.activation(out=by_z[:], in_=steeps[:, 2:5], func=ACT.Copy, scale=r)
+        half_r, neg_half_r, neg_r = [by_z[:, j : j + 1] for j in range(3)]
+        sq1 = affine("sq1", e1[:], z[:], neg_two, ACT.Square)
         gate_bias = affine("gate_bias", sum_pb[:], neg_half_r, sq0_term[:])
-        mean_b = times("mean_b", sum_pb[:], r)
         t = affine("t", sq1[:], neg_quarter, gate_bias[:], ACT.Tanh)
-        n1 = times("n1", mean_b[:], neg_half_r)
-        n2 = affine("n2", mean_b[:], neg_half_r, neg_r[:])
+        neg_mean_b = times("neg_mean_b", sum_pb[:], neg_r)
+        n1 = times("n1", neg_mean_b[:], half_r)
+        n2 = affine("n2", neg_mean_b[:], half_r, neg_r)
         d0 = affine("d0", t[:], half_r, half_r)
         d1 = affine("d1", t[:], n1[:], n2[:])
         neg_beta = times("neg_beta", d1[:], sum_pc[:])
-        gate_r = affine("gate_r", t[:], neg_r[:], r)
+        gate_r = affine("gate_r", t[:], neg_r, r)
         row_scale = times("row_scale", gate_r[:], GRAD_SCALE / 2)
 
         b_term = keep.tile([ROWS, SLOTS], F32, name="b_term")

import math
from contextlib import ExitStack

import concourse.mybir as mybir

F32 = mybir.dt.float32
BF16 = mybir.dt.bfloat16
I32 = mybir.dt.int32
U32 = mybir.dt.uint32
U16 = mybir.dt.uint16
U8 = mybir.dt.uint8
FP8X4 = mybir.dt.float8_e4m3fn_x4
ALU = mybir.AluOpType
ACT = mybir.ActivationFunctionType

P = 128
PACK = 4
TOKENS = 2048
SLOTS = 512
ROWS = 128
FLOPS = 2 * 2 * 512 * ROWS * SLOTS

GRAD_SCALE = 1024.0
LN2 = math.log(2.0)
GUESS_SLOPE = LN2 / 2.0**23
GUESS_SHIFT = 127.0 * LN2 - 0.03
STORE_WIDTHS = (256, 384, 384, 384, 384, 256)


def tile_attend_bcertainty_s_kernel(tc, query, keys_words, keys_scales, th, steep, sdot, gout,
                                     vals_words, vals_scales, old, offs, out):
    nc = tc.nc
    with ExitStack() as ctx:
        keep = ctx.enter_context(tc.tile_pool(name="keep", bufs=1))
        psum = ctx.enter_context(tc.psum_pool(name="psum", bufs=1))

        def column(name):
            return keep.tile([P, 1], F32, name=name)

        def affine(name, x, scale, bias, func=ACT.Identity):
            y = column(name)
            nc.scalar.activation(out=y[:], in_=x, func=func, scale=scale, bias=bias)
            return y

        def times(name, x, scale):
            y = column(name)
            nc.scalar.activation(out=y[:], in_=x, func=ACT.Copy, scale=scale)
            return y

        offsets = keep.tile([P, SLOTS // 16], U16, name="offsets")
        nc.sync.dma_start(offsets[:], offs)

        def load_operand(name, src):
            raw = keep.tile([P, PACK, ROWS], F32, name=name, tag=name, align_bytes=64)
            nc.sync.dma_start(out=raw[:], in_=src.rearrange("(p j) w -> p j w", j=PACK))
            return raw

        def quantize(name, tag, raw):
            grouped = keep.tile([P, ROWS, PACK], BF16, name=name + "_grouped", tag=tag, align_bytes=64)
            nc.scalar.copy(out=grouped[:], in_=raw[:].rearrange("p j w -> p w j"))
            codes = keep.tile([P, ROWS], U32, name=name + "_codes", align_bytes=64)
            scales = keep.tile([P, ROWS], U8, name=name + "_scales", align_bytes=64)
            nc.vector.quantize_mx(out=codes[:].bitcast(FP8X4), scales=scales[:],
                                  in_=grouped[:].rearrange("p w j -> p (w j)"))
            return codes, scales

        def load_words(name, tag, src):
            words = keep.tile([P, TOKENS], I32, name=name, tag=tag, align_bytes=64)
            nc.sync.dma_start(out=words[:], in_=src[0].rearrange("p n t -> p (n t)").bitcast(I32))
            return words

        def load_column(name, tag, src):
            col = keep.tile([P, 1], F32, name=name, tag=tag, align_bytes=64)
            nc.sync.dma_start(out=col[:], in_=src)
            return col

        def load_plane(name, tag, src, first):
            plane = keep.tile([P, TOKENS], U8, name=name, tag=tag)
            nc.vector.memset(plane[:].bitcast(I32), 0)
            for j in range(4):
                nc.sync.dma_start(out=plane[first + j : P : 32, :].bitcast(I32), in_=src[0, j:16:4, :].bitcast(I32))
            return plane

        def gather(name, window, dtype):
            picked = keep.tile([P, SLOTS], dtype, name=name, align_bytes=64)
            nc.vector.tensor_copy(picked[:], window.indirect(offsets[:]))
            return picked

        def product(name, stationary, words, plane):
            acc = psum.tile([ROWS, SLOTS], F32, name=name)
            nc.tensor.matmul_mx(out=acc[:], lhsT=stationary[0][:].bitcast(FP8X4), lhsT_scale=stationary[1][:],
                                rhs=words[:].bitcast(FP8X4), rhs_scale=plane, start=True, stop=True)
            return acc

        q_raw = load_operand("q_raw", query)
        g_raw = load_operand("g_raw", gout)
        one = keep.tile([P, 1], F32, name="one", tag="k_pool", align_bytes=64)
        nc.vector.memset(one[:], 1.0)
        k_plane = load_plane("k_plane", "k_plane", keys_scales, 0)

        consts = keep.tile([P, 3], F32, name="consts")
        for j, c in enumerate((-2.0, GUESS_SHIFT, GUESS_SHIFT - 0.5)):
            nc.vector.tensor_scalar(out=consts[:, j : j + 1], in0=one[:], scalar1=c, scalar2=None, op0=ALU.mult)
        neg_two, guess_e, guess_s = [consts[:, j : j + 1] for j in range(3)]
        k_pool = load_words("k_pool", "k_pool", keys_words)
        v_plane = load_plane("v_plane", "v_plane", vals_scales, 4)

        window = keep.tile([ROWS, TOKENS], F32, name="window")
        nc.vector.memset(window[:].bitcast(I32), 0)


        k_bytes = gather("k_bytes", k_plane[:], U8)
        q_mx = quantize("q", "q_grouped", q_raw)
        g_mx = quantize("g", "g_grouped", g_raw)
        steep_sb = load_column("steep_sb", "q_raw", steep)
        v_pool = load_words("v_pool", "g_raw", vals_words)
        th_sb = load_column("th_sb", "q_grouped", th)
        sdot_sb = load_column("sdot_sb", "g_grouped", sdot)
        k_words = gather("k_words", k_pool[:].bitcast(U32), U32)
        a = product("a", q_mx, k_words, k_bytes[:])
        v_bytes = gather("v_bytes", v_plane[:], U8)

        steeps = keep.tile([P, 5], F32, name="steeps")
        for j, c in enumerate((0.25, -0.25, 0.5, -0.5)):
            nc.scalar.activation(out=steeps[:, j : j + 1], in_=steep_sb[:], func=ACT.Copy, scale=c)
        nc.scalar.activation(out=steeps[:, 4:5], in_=neg_two, func=ACT.Copy, scale=0.5)
        quarter, neg_quarter, neg_half = [steeps[:, j : j + 1] for j in (0, 1, 3)]
        th_term = affine("th_term", th_sb[:], neg_half, quarter)

        neg_max = keep.tile([P, 1], F32, name="neg_max", tag="v_plane")
        nc.vector.tensor_reduce(out=neg_max[:], in_=a[:], axis=mybir.AxisListType.X, op=ALU.max, negate=True)
        p = keep.tile([ROWS, SLOTS], F32, name="p", tag="q_raw", align_bytes=64)
        z = column("z")
        nc.scalar.activation(out=p[:], in_=a[:], func=ACT.Exp, bias=neg_max[:], scale=1.0, accum_out=z[:])

        v_words = gather("v_words", v_pool[:].bitcast(U32), U32)
        c0 = product("c0", g_mx, v_words, v_bytes[4:P, :])
        old_sb = keep.tile([ROWS, TOKENS], F32, name="old_sb", tag="k_pool", align_bytes=64)
        nc.sync.dma_start(out=old_sb[:], in_=old)

        pb_r = keep.tile([ROWS, SLOTS + 1], F32, name="pb_r", tag="g_raw", align_bytes=64)
        pb, r = pb_r[:, :SLOTS], pb_r[:, SLOTS:]
        nc.vector.reciprocal(out=r, in_=z[:])
        sum_pb = column("sum_pb")
        nc.vector.scalar_tensor_tensor(out=pb, in0=a[:], scalar=neg_max[:], in1=p[:], op0=ALU.add,
                                       op1=ALU.mult, accum_out=sum_pb[:])
        pc = keep.tile([ROWS, SLOTS], F32, name="pc")
        sum_pc = column("sum_pc")
        nc.vector.scalar_tensor_tensor(out=pc[:], in0=c0[:], scalar=sdot_sb[:], in1=p[:],
                                       op0=ALU.subtract, op1=ALU.mult, accum_out=sum_pc[:])

        z_bits = z[:].bitcast(U32)
        e0 = affine("e0", z_bits, -GUESS_SLOPE, guess_e, ACT.Exp)
        shift = affine("shift", z_bits, -GUESS_SLOPE, guess_s)
        sq0 = affine("sq0", e0[:], z[:], neg_two, ACT.Square)
        shift_term = affine("shift_term", shift[:], neg_half, th_term[:])
        e1 = affine("e1", sq0[:], 0.5, shift[:], ACT.Exp)
        sq0_term = affine("sq0_term", sq0[:], neg_quarter, shift_term[:])
        by_z = keep.tile([P, 3], F32, name="by_z")
        nc.scalar.activation(out=by_z[:], in_=steeps[:, 2:5], func=ACT.Copy, scale=r)
        half_r, neg_half_r, neg_r = [by_z[:, j : j + 1] for j in range(3)]
        sq1 = affine("sq1", e1[:], z[:], neg_two, ACT.Square)
        gate_bias = affine("gate_bias", sum_pb[:], neg_half_r, sq0_term[:])
        t = affine("t", sq1[:], neg_quarter, gate_bias[:], ACT.Tanh)
        neg_mean_b = times("neg_mean_b", sum_pb[:], neg_r)
        n1 = times("n1", neg_mean_b[:], half_r)
        n2 = affine("n2", neg_mean_b[:], half_r, neg_r)
        d0 = affine("d0", t[:], half_r, half_r)
        d1 = affine("d1", t[:], n1[:], n2[:])
        neg_beta = times("neg_beta", d1[:], sum_pc[:])
        gate_r = affine("gate_r", t[:], neg_r, r)
        row_scale = times("row_scale", gate_r[:], GRAD_SCALE / 2)

        b_term = keep.tile([ROWS, SLOTS], F32, name="b_term")
        nc.vector.tensor_scalar(out=b_term[:], in0=pb, scalar1=d0[:], scalar2=sum_pc[:], op0=ALU.mult, op1=ALU.mult)
        c_term = keep.tile([ROWS, SLOTS], F32, name="c_term")
        nc.vector.scalar_tensor_tensor(out=c_term[:], in0=p[:], scalar=neg_beta[:], in1=pc[:], op0=ALU.mult, op1=ALU.add)
        nc.vector.tensor_tensor(window[:].indirect(offsets[:]), b_term[:], c_term[:], ALU.add)

        start = 0
        for i, width in enumerate(STORE_WIDTHS):
            cols = slice(start, start + width)
            start = start + width
            result = keep.tile([ROWS, width], F32, name="result%d" % i)
            nc.vector.scalar_tensor_tensor(out=result[:], in0=window[:, cols], scalar=row_scale[:],
                                           in1=old_sb[:, cols], op0=ALU.mult, op1=ALU.add)
            queue = nc.sync if i % 2 == 0 else nc.scalar
            queue.dma_start(out=out[:, cols], in_=result[:])
